import numpy as np
import ml_dtypes


def mxq(x, axis, fmt="e4m3"):
    dtype, down = {"e4m3": (ml_dtypes.float8_e4m3fn, 7), "e5m2": (ml_dtypes.float8_e5m2, 14)}[fmt]
    v = np.moveaxis(np.asarray(x, np.float32).astype(ml_dtypes.bfloat16).astype(np.float64), axis, -1)
    blocks = v.reshape(v.shape[:-1] + (-1, 32))
    amax = np.abs(blocks).max(-1, keepdims=True)
    byte = np.maximum(np.where(amax > 0, np.frexp(amax)[1] - 1 + 127, 0) - down, 1)
    scale = np.exp2(byte - 127.0)
    codes = (blocks / scale).astype(np.float32).astype(dtype).astype(np.float64)
    return np.moveaxis((codes * scale).reshape(v.shape), -1, axis)


WIDE = False


def mx_kscale(k):
    if not WIDE:
        return np.ones(k)
    levels = np.array([10, -10, 5, -5, 0])
    if k % 512:
        return np.exp2(np.random.permutation(np.resize(levels, k // 32))).repeat(32)
    a = np.empty((k // 512, 16))
    for p in range(k // 512):
        a[p, :8] = np.random.permutation(np.resize(levels, 8))
        for g in range(8):
            far = levels[np.abs(levels - a[p, g]) >= 10]
            a[p, g + 8] = far[np.random.randint(len(far))]
    return np.exp2(a.ravel()).repeat(32)


def f64(x):
    return np.asarray(x).astype(np.float64)


def striped(idx):
    return np.tile(idx.reshape(-1, 16).T, (8, 1)).astype(np.uint16)


def unstriped(offs):
    return offs[:16].T.reshape(-1).astype(np.int64)


def striped8(idx):
    return np.concatenate([x.reshape(-1, 16).T for x in idx]).astype(np.uint16)


def runs(offs, k):
    lists = np.stack([offs[16 * r : 16 * r + 16].T.reshape(-1) for r in range(8)]).astype(np.int64)
    return lists[np.arange(k) % 512 // 64]


def pack_weight(w):
    k, n = w.shape
    w = f64(np.asarray(w, np.float32).astype(ml_dtypes.bfloat16)).reshape(k // 32, 32, n)
    amax = np.abs(w).max(1)
    byte = np.clip(np.where(amax > 0, np.frexp(amax)[1] - 1 + 127 - 7, 1), 1, 254)
    scaled = (w * np.exp2(127.0 - byte)[:, None, :]).reshape(k, n).astype(np.float32)
    words = np.ascontiguousarray(scaled.reshape(k // 512, 128, 4, n).transpose(0, 1, 3, 2)).astype(ml_dtypes.float8_e4m3fn).view(np.uint8)
    return words, np.ascontiguousarray(byte.astype(np.uint8).reshape(k // 512, 16, n))


def unpack_weight(words, scales):
    g, p, n, _ = words.shape
    vals = np.ascontiguousarray(words).view(ml_dtypes.float8_e4m3fn).astype(np.float64) * np.repeat(np.exp2(scales.astype(np.float64) - 127.0), 8, axis=1)[..., None]
    return vals.transpose(0, 1, 3, 2).reshape(g * 512, n)


def sigmoid(v):
    return 1.0 / (1.0 + np.exp(-np.maximum(v, -700.0)))


K, T, S, N, G, H = 512, 1024, 512, 512, 2048, 512


def setup_inputs():
    n = np.random.standard_normal
    s = mx_kscale(K)[:, None]
    u = mx_kscale(S)
    packed_xT = pack_weight(n((K, T)) * s)
    packed_dT = pack_weight(n((K, G)) / s)
    return {
        "x_words": packed_xT[0],
        "x_scales": packed_xT[1],
        "d_words": packed_dT[0],
        "d_scales": packed_dT[1],
        "gn": (np.random.uniform(0.5, 1.5, (H, 1)) * u[:, None]).astype(np.float32),
        "w1": (n((H, N)) / np.sqrt(H) / u[:, None]).astype(np.float32),
        "offs": striped(np.random.permutation(T)[:S]),
        "k1": striped8(np.random.randint(0, G, (8, H))),
        "two": striped(np.random.permutation(T)[:S]),
        "k2": striped8(np.random.randint(0, G, (8, H))),
        "n1": striped(np.random.permutation(S)),
        "n2": striped(np.random.permutation(S)),
        "n3": striped8(np.stack([np.random.permutation(S) for _ in range(8)])),
    }


def reference(x_words, x_scales, d_words, d_scales, gn, w1, offs, k1, two, k2, n1, n2, n3):
    d_k1 = unpack_weight(d_words, d_scales)[np.arange(K)[:, None], runs(k1, K)]
    xq = unpack_weight(x_words, x_scales)[:, unstriped(offs)]
    a = 0.0625 * (d_k1.T @ xq)
    d_k2 = unpack_weight(d_words, d_scales)[np.arange(K)[:, None], runs(k2, K)]
    x_two = unpack_weight(x_words, x_scales)[:, unstriped(two)]
    b = 0.0625 * (d_k2.T @ x_two)
    z = f64(gn) * (a * (sigmoid(b[:, unstriped(n2)])) - (0.5 * a[:, unstriped(n1)]))
    h = mxq(f64(w1), 0, "e4m3").T @ mxq(z, 0, "e4m3")
    return h / (np.abs(h[np.arange(N)[:, None], runs(n3, N)]) + 0.5)

@@ -1,0 +1,221 @@
+from contextlib import ExitStack
+
+import concourse.mybir as mybir
+
+F32 = mybir.dt.float32
+BF16 = mybir.dt.bfloat16
+I32 = mybir.dt.int32
+U32 = mybir.dt.uint32
+U16 = mybir.dt.uint16
+U8 = mybir.dt.uint8
+FP8X4 = mybir.dt.float8_e4m3fn_x4
+ACT = mybir.ActivationFunctionType
+ALU = mybir.AluOpType
+
+P = 128
+S = 512
+HALF = S // 2
+TILES = 4
+FLOPS = 3 * 2 * 512 * 512 * 512
+
+
+def tile_picked_twpqgatebnorm_none_p_kernel(
+    tc, x_words, x_scales, d_words, d_scales, gn, w1, offs, k1, two, k2, n1, n2, n3, out
+):
+    nc = tc.nc
+    tokens = x_words.shape[2]
+    codewords = d_words.shape[2]
+
+    with ExitStack() as ctx:
+        sb = ctx.enter_context(tc.tile_pool(name="sb", bufs=1))
+        psum = ctx.enter_context(tc.psum_pool(name="psum", bufs=1))
+
+        def tile(name, shape, dtype, tag=None):
+            return sb.tile(shape, dtype, name=name, tag=tag or name, align_bytes=64)
+
+        def load_list(name, src):
+            dst = sb.tile([P, S // 16], U16, name=name)
+            nc.sync.dma_start(dst[:], src)
+            return dst
+
+        def load_scale_rows(name, src, width):
+            dst = tile(name, [P, width], U8)
+            rows = src[0].bitcast(I32).rearrange("q (o c) -> q o c", o=1)
+            nc.sync.dma_start(dst[:].bitcast(I32), rows.to_broadcast([16, 8, width // 4]))
+            return dst
+
+        def load_words(name, src, width):
+            dst = tile(name, [P, width], U32)
+            nc.sync.dma_start(dst[:].bitcast(I32), src[0].rearrange("p c r -> p (c r)").bitcast(I32))
+            return dst
+
+        def half_of(lst, half):
+            return lst[:, half * (HALF // 16) : (half + 1) * (HALF // 16)]
+
+        def cols(half):
+            return slice(half * HALF, (half + 1) * HALF)
+
+        planes = tile("planes", [P, 4 * S], U8)
+        nc.gpsimd.memset(planes[:].bitcast(I32), 0)
+
+        two_l = load_list("two_l", two)
+        x_bytes = load_scale_rows("x_bytes", x_scales, tokens)
+        offs_l = load_list("offs_l", offs)
+        d_bytes = load_scale_rows("d_bytes", d_scales, codewords)
+        k2_l = load_list("k2_l", k2)
+        k1_l = load_list("k1_l", k1)
+        x_table = load_words("x_table", x_words, tokens)
+        d_table = load_words("d_table", d_words, codewords)
+        w_raw = tile("w_raw", [P, TILES, S], F32)
+        w_rows = w1.rearrange("(g t r) m -> t g r m", t=TILES, r=8)
+        for t in range(TILES):
+            nc.sync.dma_start(w_raw[:, t, :], w_rows[t])
+        n2_l = load_list("n2_l", n2)
+        n1_l = load_list("n1_l", n1)
+        n3_l = load_list("n3_l", n3)
+
+        gain_raw = tile("gain_raw", [P, TILES, 8], F32)
+        gain_rows = gn.rearrange("(g t r) o -> t g r o", t=TILES, r=8)
+        with nc.allow_non_contiguous_dma(reason="one gain a partition"):
+            for t in range(TILES):
+                nc.gpsimd.dma_start(gain_raw[:, t, 0:1], gain_rows[t])
+
+        d_bytes_picked = tile("d_bytes_picked", [P, 2 * S], U8)
+        x_bytes_picked = tile("x_bytes_picked", [P, 2 * S], U8)
+        nc.vector.tensor_copy(x_bytes_picked[:, 0:S], x_bytes[:].indirect(two_l[:]))
+        nc.vector.tensor_copy(x_bytes_picked[:, S : 2 * S], x_bytes[:].indirect(offs_l[:]))
+        nc.vector.tensor_copy(d_bytes_picked[:, 0:S], d_bytes[:].indirect(k2_l[:]))
+        nc.vector.tensor_copy(d_bytes_picked[:, S : 2 * S], d_bytes[:].indirect(k1_l[:]))
+        staged = tile("staged", [P, 4 * S], U8)
+        nc.vector.tensor_copy(
+            staged[:, 0 : 2 * S].bitcast(I32).rearrange("p (l t g r) -> p l t g r", l=2, t=TILES, r=2),
+            d_bytes_picked[:].bitcast(I32).rearrange("p (l g t r) -> p l t g r", l=2, t=TILES, r=2),
+        )
+        nc.vector.tensor_copy(staged[:, 2 * S : 4 * S].bitcast(I32), x_bytes_picked[:].bitcast(I32))
+        for q in range(4):
+            nc.sync.dma_start(
+                planes[32 * q : 32 * q + 4, :].bitcast(I32),
+                staged[32 * q : 32 * q + 32 : 8, :].bitcast(I32),
+            )
+
+        gain = tile("gain", [P, TILES], F32)
+        nc.gpsimd.tensor_scalar(gain[:], gain_raw[:, :, 0], 0.0625, 0.0, ALU.mult, ALU.add)
+
+        def coded_layer(which, name, d_list, x_list, d_tag, x_tag):
+            x_picked = tile(name + "_x", [P, S], U32, x_tag)
+            d_picked = tile(name + "_d", [P, S], U32, d_tag)
+            d_dealt = tile(name + "_dealt", [P, S], U32)
+            nc.vector.tensor_copy(x_picked[:], x_table[:].indirect(x_list[:]))
+            nc.vector.tensor_copy(d_picked[:], d_table[:].indirect(d_list[:]))
+            nc.vector.tensor_copy(
+                d_dealt[:].rearrange("p (t g r) -> p t g r", t=TILES, r=8),
+                d_picked[:].rearrange("p (g t r) -> p t g r", t=TILES, r=8),
+            )
+            banks = []
+            for t in range(TILES):
+                bank = psum.tile([P, S], F32, name=name + str(t), tag="bank" + str(TILES * which + t))
+                nc.tensor.matmul_mx(
+                    out=bank[:],
+                    lhsT=d_dealt[:, P * t : P * (t + 1)].bitcast(FP8X4),
+                    lhsT_scale=planes[:, which * S + P * t : which * S + P * (t + 1)],
+                    rhs=x_picked[:].bitcast(FP8X4),
+                    rhs_scale=planes[:, (2 + which) * S : (3 + which) * S],
+                    start=True,
+                    stop=True,
+                )
+                banks.append(bank)
+            return banks
+
+        w_bf = tile("w_bf", [P, TILES * S], BF16)
+        w_src = w_raw[:].rearrange("p t (g u h i) -> p u g h t i", u=TILES, h=2, i=4)
+        for u in range(TILES):
+            nc.scalar.copy(
+                w_bf[:, u * S : (u + 1) * S].rearrange("p (g h i t) -> p g h t i", h=2, i=4, t=TILES),
+                w_src[:, u],
+            )
+
+        b_banks = coded_layer(0, "b", k2_l, two_l, "b_d", "b_x")
+        gate = [tile("gate" + str(t), [P, S], F32) for t in range(TILES)]
+        for t in range(TILES):
+            nc.scalar.activation(gate[t][:], b_banks[t][:], ACT.Sigmoid, scale=0.0625)
+
+        a_banks = coded_layer(1, "a", k1_l, offs_l, "b_d", "staged")
+        w_codes = tile("w_codes", [P, S], U32)
+        w_scales = tile("w_scales", [P, S], U8)
+        nc.vector.quantize_mx(out=w_codes[:].bitcast(FP8X4), scales=w_scales[:], in_=w_bf[:])
+        ga = [tile("ga" + str(t), [P, S], F32) for t in range(TILES)]
+        nc.vector.tensor_scalar(ga[0][:], a_banks[0][:], gain[:, 0:1], None, ALU.mult)
+        for t in range(1, TILES):
+            nc.scalar.activation(ga[t][:], a_banks[t][:], ACT.Copy, scale=gain[:, t : t + 1])
+
+        gated = [tile("gated" + str(half), [P, TILES, HALF], F32) for half in range(2)]
+        other = [tile("other" + str(half), [P, TILES, HALF], F32) for half in range(2)]
+        for half in range(2):
+            for t in range(TILES):
+                nc.scalar.activation(other[half][:, t, :], ga[t][:].indirect(half_of(n1_l, half)), ACT.Copy, scale=-0.5)
+        for half in range(2):
+            for t in range(TILES):
+                nc.vector.tensor_tensor(
+                    gated[half][:, t, :], gate[t][:].indirect(half_of(n2_l, half)), ga[t][:, cols(half)], ALU.mult
+                )
+
+        h_banks = [psum.tile([P, S], F32, name="h" + str(u), tag="bank" + str(u)) for u in range(TILES)]
+        for half in range(2):
+            z_bf = tile("z_bf" + str(half), [P, TILES * HALF], BF16, "z_bf")
+            nc.vector.tensor_tensor(
+                z_bf[:].rearrange("p (c i t) -> p c t i", i=4, t=TILES),
+                gated[half][:].rearrange("p t (c i) -> p c t i", i=4),
+                other[half][:].rearrange("p t (c i) -> p c t i", i=4),
+                ALU.add,
+            )
+            z_codes = tile("z_codes" + str(half), [P, HALF], U32)
+            z_scales = tile("z_scales" + str(half), [P, HALF], U8)
+            nc.vector.quantize_mx(out=z_codes[:].bitcast(FP8X4), scales=z_scales[:], in_=z_bf[:])
+            for u in range(TILES):
+                nc.tensor.matmul_mx(
+                    out=h_banks[u][:, cols(half)],
+                    lhsT=w_codes[:, P * u : P * (u + 1)].bitcast(FP8X4),
+                    lhsT_scale=w_scales[:, P * u : P * (u + 1)],
+                    rhs=z_codes[:].bitcast(FP8X4),
+                    rhs_scale=z_scales[:],
+                    start=True,
+                    stop=True,
+                )
+
+        size = [tile("size" + str(u), [P, S], F32) for u in range(TILES)]
+        root = [tile("root" + str(u), [P, S], F32) for u in range(TILES)]
+        inv = [tile("inv" + str(u), [P, S], F32) for u in range(TILES)]
+        side = [tile("side" + str(u), [P, S], F32) for u in range(TILES)]
+        res = [tile("res" + str(u), [P, S], F32) for u in range(TILES)]
+        out_rows = out.rearrange("(g u r) j -> u g r j", u=TILES, r=8)
+
+        def inverse_root(u):
+            nc.scalar.activation(size[u][:], h_banks[u][:], ACT.Abs)
+            nc.scalar.activation(root[u][:], size[u][:], ACT.Abs_reciprocal_sqrt, bias=0.5)
+
+        def finish_on_vector(u):
+            for half in range(2):
+                nc.vector.tensor_tensor(
+                    res[u][:, cols(half)], inv[u][:].indirect(half_of(n3_l, half)), side[u][:, cols(half)], ALU.mult
+                )
+            nc.sync.dma_start(out_rows[u], res[u][:])
+
+        nc.vector.tensor_copy(side[1][:], h_banks[1][:])
+        inverse_root(0)
+        nc.vector.tensor_copy(side[0][:], h_banks[0][:])
+        nc.vector.tensor_copy(side[2][:], h_banks[2][:])
+        inverse_root(1)
+        for u in range(2):
+            nc.vector.tensor_tensor(inv[u][:], root[u][:], root[u][:], ALU.mult)
+            finish_on_vector(u)
+        for u in range(2, TILES):
+            inverse_root(u)
+            nc.scalar.activation(inv[u][:], root[u][:], ACT.Square)
+        finish_on_vector(2)
+        last = TILES - 1
+        for half in range(2):
+            nc.scalar.activation(side[last][:, cols(half)], inv[last][:].indirect(half_of(n3_l, half)), ACT.Copy)
+            nc.vector.tensor_tensor(
+                res[last][:, cols(half)], h_banks[last][:, cols(half)], side[last][:, cols(half)], ALU.mult
+            )
+        nc.sync.dma_start(out_rows[last], res[last][:])

@@ -58,6 +58,10 @@ def tile_picked_twpqgatebnorm_none_p_kernel(
         planes = tile("planes", [P, 4 * S], U8)
         nc.gpsimd.memset(planes[:].bitcast(I32), 0)
 
+        warm = tile("warm", [P, 24], F32)
+        nc.gpsimd.memset(warm[:, 0:1], 0.0)
+        nc.scalar.activation(warm[:, 8:9], warm[:, 0:1], ACT.Sigmoid)
+
         two_l = load_list("two_l", two)
         x_bytes = load_scale_rows("x_bytes", x_scales, tokens)
         offs_l = load_list("offs_l", offs)
@@ -159,6 +163,7 @@ def tile_picked_twpqgatebnorm_none_p_kernel(
                     gated[half][:, t, :], gate[t][:].indirect(half_of(n2_l, half)), ga[t][:, cols(half)], ALU.mult
                 )
 
+        nc.scalar.activation(warm[:, 16:17], other[1][:, TILES - 1, HALF - 1 : HALF], ACT.Abs_reciprocal_sqrt, bias=0.5)
         h_banks = [psum.tile([P, S], F32, name="h" + str(u), tag="bank" + str(u)) for u in range(TILES)]
         for half in range(2):
             z_bf = tile("z_bf" + str(half), [P, TILES * HALF], BF16, "z_bf")

@@ -16,6 +16,7 @@ P = 128
 S = 512
 HALF = S // 2
 TILES = 4
+EARLY = 2
 FLOPS = 3 * 2 * 512 * 512 * 512
 
 
@@ -70,13 +71,13 @@ def tile_picked_twpqgatebnorm_none_p_kernel(
         k1_l = load_list("k1_l", k1)
         x_table = load_words("x_table", x_words, tokens)
         d_table = load_words("d_table", d_words, codewords)
+        n2_l = load_list("n2_l", n2)
+        n1_l = load_list("n1_l", n1)
+        n3_l = load_list("n3_l", n3)
         w_raw = tile("w_raw", [P, TILES, S], F32)
         w_rows = w1.rearrange("(g t r) m -> t g r m", t=TILES, r=8)
         for t in range(TILES):
             nc.sync.dma_start(w_raw[:, t, :], w_rows[t])
-        n2_l = load_list("n2_l", n2)
-        n1_l = load_list("n1_l", n1)
-        n3_l = load_list("n3_l", n3)
 
         gain_raw = tile("gain_raw", [P, TILES, 8], F32)
         gain_rows = gn.rearrange("(g t r) o -> t g r o", t=TILES, r=8)
@@ -131,10 +132,10 @@ def tile_picked_twpqgatebnorm_none_p_kernel(
             return banks
 
         w_bf = tile("w_bf", [P, TILES * S], BF16)
-        w_src = w_raw[:].rearrange("p t (g u h i) -> p u g h t i", u=TILES, h=2, i=4)
+        w_src = w_raw[:].rearrange("p t (g u h i) -> p u g h t i", u=TILES, h=4, i=2)
         for u in range(TILES):
             nc.scalar.copy(
-                w_bf[:, u * S : (u + 1) * S].rearrange("p (g h i t) -> p g h t i", h=2, i=4, t=TILES),
+                w_bf[:, u * S : (u + 1) * S].rearrange("p (g h i t) -> p g h t i", h=4, i=2, t=TILES),
                 w_src[:, u],
             )
 
@@ -164,13 +165,17 @@ def tile_picked_twpqgatebnorm_none_p_kernel(
                 )
 
         nc.scalar.activation(warm[:, 16:17], other[1][:, TILES - 1, HALF - 1 : HALF], ACT.Abs_reciprocal_sqrt, bias=0.5)
-        h_banks = [psum.tile([P, S], F32, name="h" + str(u), tag="bank" + str(u)) for u in range(TILES)]
+        h_psum = []
+        for u in range(TILES):
+            first = psum.tile([P, S], F32, name="h" + str(u), tag="bank" + str(u))
+            second = psum.tile([P, S], F32, name="hh" + str(u), tag="bank" + str(TILES + u)) if u < EARLY else first
+            h_psum.append([first, second])
         for half in range(2):
             z_bf = tile("z_bf" + str(half), [P, TILES * HALF], BF16, "z_bf")
             nc.vector.tensor_tensor(
-                z_bf[:].rearrange("p (c i t) -> p c t i", i=4, t=TILES),
-                gated[half][:].rearrange("p t (c i) -> p c t i", i=4),
-                other[half][:].rearrange("p t (c i) -> p c t i", i=4),
+                z_bf[:].rearrange("p (c i t) -> p c t i", i=2, t=TILES),
+                gated[half][:].rearrange("p t (c i) -> p c t i", i=2),
+                other[half][:].rearrange("p t (c i) -> p c t i", i=2),
                 ALU.add,
             )
             z_codes = tile("z_codes" + str(half), [P, HALF], U32)
@@ -178,7 +183,7 @@ def tile_picked_twpqgatebnorm_none_p_kernel(
             nc.vector.quantize_mx(out=z_codes[:].bitcast(FP8X4), scales=z_scales[:], in_=z_bf[:])
             for u in range(TILES):
                 nc.tensor.matmul_mx(
-                    out=h_banks[u][:, cols(half)],
+                    out=h_psum[u][half][:, cols(half)],
                     lhsT=w_codes[:, P * u : P * (u + 1)].bitcast(FP8X4),
                     lhsT_scale=w_scales[:, P * u : P * (u + 1)],
                     rhs=z_codes[:].bitcast(FP8X4),
@@ -194,9 +199,9 @@ def tile_picked_twpqgatebnorm_none_p_kernel(
         res = [tile("res" + str(u), [P, S], F32) for u in range(TILES)]
         out_rows = out.rearrange("(g u r) j -> u g r j", u=TILES, r=8)
 
-        def inverse_root(u):
-            nc.scalar.activation(size[u][:], h_banks[u][:], ACT.Abs)
-            nc.scalar.activation(root[u][:], size[u][:], ACT.Abs_reciprocal_sqrt, bias=0.5)
+        def inverse_root(u, bank, span):
+            nc.scalar.activation(size[u][:, span], bank[:, span], ACT.Abs)
+            nc.scalar.activation(root[u][:, span], size[u][:, span], ACT.Abs_reciprocal_sqrt, bias=0.5)
 
         def finish_on_vector(u):
             for half in range(2):
@@ -205,22 +210,22 @@ def tile_picked_twpqgatebnorm_none_p_kernel(
                 )
             nc.sync.dma_start(out_rows[u], res[u][:])
 
-        nc.vector.tensor_copy(side[1][:], h_banks[1][:])
-        inverse_root(0)
-        nc.vector.tensor_copy(side[0][:], h_banks[0][:])
-        nc.vector.tensor_copy(side[2][:], h_banks[2][:])
-        inverse_root(1)
-        for u in range(2):
+        for half in range(2):
+            for u in range(EARLY):
+                inverse_root(u, h_psum[u][half], cols(half))
+                nc.vector.tensor_copy(side[u][:, cols(half)], h_psum[u][half][:, cols(half)])
+        nc.vector.tensor_copy(side[2][:], h_psum[2][0][:])
+        for u in range(EARLY):
             nc.vector.tensor_tensor(inv[u][:], root[u][:], root[u][:], ALU.mult)
             finish_on_vector(u)
-        for u in range(2, TILES):
-            inverse_root(u)
+        for u in range(EARLY, TILES):
+            inverse_root(u, h_psum[u][0], slice(0, S))
             nc.scalar.activation(inv[u][:], root[u][:], ACT.Square)
         finish_on_vector(2)
         last = TILES - 1
         for half in range(2):
             nc.scalar.activation(side[last][:, cols(half)], inv[last][:].indirect(half_of(n3_l, half)), ACT.Copy)
             nc.vector.tensor_tensor(
-                res[last][:, cols(half)], h_banks[last][:, cols(half)], side[last][:, cols(half)], ALU.mult
+                res[last][:, cols(half)], h_psum[last][0][:, cols(half)], side[last][:, cols(half)], ALU.mult
             )
-        nc.sync.dma_start(out_rows[last], res[last][:])
+            nc.sync.dma_start(out_rows[last][:, :, cols(half)], res[last][:, cols(half)])

@@ -17,6 +17,7 @@ S = 512
 HALF = S // 2
 TILES = 4
 EARLY = 2
+SPARE = 32
 FLOPS = 3 * 2 * 512 * 512 * 512
 
 
@@ -50,6 +51,11 @@ def tile_picked_twpqgatebnorm_none_p_kernel(
             nc.sync.dma_start(dst[:].bitcast(I32), src[0].rearrange("p c r -> p (c r)").bitcast(I32))
             return dst
 
+        def window(name):
+            dst = tile(name, [P, S + SPARE], F32)
+            nc.vector.memset(dst[:, S:], 0.0)
+            return dst
+
         def half_of(lst, half):
             return lst[:, half * (HALF // 16) : (half + 1) * (HALF // 16)]
 
@@ -57,10 +63,10 @@ def tile_picked_twpqgatebnorm_none_p_kernel(
             return slice(half * HALF, (half + 1) * HALF)
 
         planes = tile("planes", [P, 4 * S], U8)
-        nc.gpsimd.memset(planes[:].bitcast(I32), 0)
+        nc.vector.memset(planes[:].bitcast(I32), 0)
 
         warm = tile("warm", [P, 24], F32)
-        nc.gpsimd.memset(warm[:, 0:1], 0.0)
+        nc.vector.memset(warm[:, 0:1], 0.0)
         nc.scalar.activation(warm[:, 8:9], warm[:, 0:1], ACT.Sigmoid)
 
         two_l = load_list("two_l", two)
@@ -71,19 +77,19 @@ def tile_picked_twpqgatebnorm_none_p_kernel(
         k1_l = load_list("k1_l", k1)
         x_table = load_words("x_table", x_words, tokens)
         d_table = load_words("d_table", d_words, codewords)
-        n2_l = load_list("n2_l", n2)
-        n1_l = load_list("n1_l", n1)
-        n3_l = load_list("n3_l", n3)
         w_raw = tile("w_raw", [P, TILES, S], F32)
         w_rows = w1.rearrange("(g t r) m -> t g r m", t=TILES, r=8)
-        for t in range(TILES):
+        for t in range(TILES - 1):
             nc.sync.dma_start(w_raw[:, t, :], w_rows[t])
-
         gain_raw = tile("gain_raw", [P, TILES, 8], F32)
         gain_rows = gn.rearrange("(g t r) o -> t g r o", t=TILES, r=8)
         with nc.allow_non_contiguous_dma(reason="one gain a partition"):
             for t in range(TILES):
-                nc.gpsimd.dma_start(gain_raw[:, t, 0:1], gain_rows[t])
+                nc.sync.dma_start(gain_raw[:, t, 0:1], gain_rows[t])
+        nc.sync.dma_start(w_raw[:, TILES - 1, :], w_rows[TILES - 1])
+        n2_l = load_list("n2_l", n2)
+        n1_l = load_list("n1_l", n1)
+        n3_l = load_list("n3_l", n3)
 
         d_bytes_picked = tile("d_bytes_picked", [P, 2 * S], U8)
         x_bytes_picked = tile("x_bytes_picked", [P, 2 * S], U8)
@@ -104,7 +110,7 @@ def tile_picked_twpqgatebnorm_none_p_kernel(
             )
 
         gain = tile("gain", [P, TILES], F32)
-        nc.gpsimd.tensor_scalar(gain[:], gain_raw[:, :, 0], 0.0625, 0.0, ALU.mult, ALU.add)
+        nc.scalar.activation(gain[:], gain_raw[:, :, 0], ACT.Copy, scale=0.0625)
 
         def coded_layer(which, name, d_list, x_list, d_tag, x_tag):
             x_picked = tile(name + "_x", [P, S], U32, x_tag)
@@ -140,29 +146,25 @@ def tile_picked_twpqgatebnorm_none_p_kernel(
             )
 
         b_banks = coded_layer(0, "b", k2_l, two_l, "b_d", "b_x")
-        gate = [tile("gate" + str(t), [P, S], F32) for t in range(TILES)]
+        gate = [window("gate" + str(t)) for t in range(TILES)]
         for t in range(TILES):
-            nc.scalar.activation(gate[t][:], b_banks[t][:], ACT.Sigmoid, scale=0.0625)
+            nc.scalar.activation(gate[t][:, 0:S], b_banks[t][:], ACT.Sigmoid, scale=0.0625)
 
         a_banks = coded_layer(1, "a", k1_l, offs_l, "b_d", "staged")
         w_codes = tile("w_codes", [P, S], U32)
         w_scales = tile("w_scales", [P, S], U8)
         nc.vector.quantize_mx(out=w_codes[:].bitcast(FP8X4), scales=w_scales[:], in_=w_bf[:])
         ga = [tile("ga" + str(t), [P, S], F32) for t in range(TILES)]
-        nc.vector.tensor_scalar(ga[0][:], a_banks[0][:], gain[:, 0:1], None, ALU.mult)
-        for t in range(1, TILES):
+        for t in range(TILES):
             nc.scalar.activation(ga[t][:], a_banks[t][:], ACT.Copy, scale=gain[:, t : t + 1])
 
-        gated = [tile("gated" + str(half), [P, TILES, HALF], F32) for half in range(2)]
+        gated = tile("gated", [P, TILES, S], F32)
         other = [tile("other" + str(half), [P, TILES, HALF], F32) for half in range(2)]
         for half in range(2):
             for t in range(TILES):
                 nc.scalar.activation(other[half][:, t, :], ga[t][:].indirect(half_of(n1_l, half)), ACT.Copy, scale=-0.5)
-        for half in range(2):
-            for t in range(TILES):
-                nc.vector.tensor_tensor(
-                    gated[half][:, t, :], gate[t][:].indirect(half_of(n2_l, half)), ga[t][:, cols(half)], ALU.mult
-                )
+        for t in range(TILES):
+            nc.vector.tensor_tensor(gated[:, t, :], gate[t][:].indirect(n2_l[:]), ga[t][:], ALU.mult)
 
         nc.scalar.activation(warm[:, 16:17], other[1][:, TILES - 1, HALF - 1 : HALF], ACT.Abs_reciprocal_sqrt, bias=0.5)
         h_psum = []
@@ -174,7 +176,7 @@ def tile_picked_twpqgatebnorm_none_p_kernel(
             z_bf = tile("z_bf" + str(half), [P, TILES * HALF], BF16, "z_bf")
             nc.vector.tensor_tensor(
                 z_bf[:].rearrange("p (c i t) -> p c t i", i=2, t=TILES),
-                gated[half][:].rearrange("p t (c i) -> p c t i", i=2),
+                gated[:, :, cols(half)].rearrange("p t (c i) -> p c t i", i=2),
                 other[half][:].rearrange("p t (c i) -> p c t i", i=2),
                 ALU.add,
             )
@@ -192,9 +194,9 @@ def tile_picked_twpqgatebnorm_none_p_kernel(
                     stop=True,
                 )
 
-        size = [tile("size" + str(u), [P, S], F32) for u in range(TILES)]
         root = [tile("root" + str(u), [P, S], F32) for u in range(TILES)]
-        inv = [tile("inv" + str(u), [P, S], F32) for u in range(TILES)]
+        inv = [tile("inv" + str(u), [P, 2 * S], F32) for u in range(TILES)]
+        size = [inv[u][:, S : 2 * S] for u in range(TILES)]
         side = [tile("side" + str(u), [P, S], F32) for u in range(TILES)]
         res = [tile("res" + str(u), [P, S], F32) for u in range(TILES)]
         out_rows = out.rearrange("(g u r) j -> u g r j", u=TILES, r=8)
@@ -204,10 +206,7 @@ def tile_picked_twpqgatebnorm_none_p_kernel(
             nc.scalar.activation(root[u][:, span], size[u][:, span], ACT.Abs_reciprocal_sqrt, bias=0.5)
 
         def finish_on_vector(u):
-            for half in range(2):
-                nc.vector.tensor_tensor(
-                    res[u][:, cols(half)], inv[u][:].indirect(half_of(n3_l, half)), side[u][:, cols(half)], ALU.mult
-                )
+            nc.vector.tensor_tensor(res[u][:], inv[u][:].indirect(n3_l[:]), side[u][:], ALU.mult)
             nc.sync.dma_start(out_rows[u], res[u][:])
 
         for half in range(2):
@@ -216,11 +215,11 @@ def tile_picked_twpqgatebnorm_none_p_kernel(
                 nc.vector.tensor_copy(side[u][:, cols(half)], h_psum[u][half][:, cols(half)])
         nc.vector.tensor_copy(side[2][:], h_psum[2][0][:])
         for u in range(EARLY):
-            nc.vector.tensor_tensor(inv[u][:], root[u][:], root[u][:], ALU.mult)
+            nc.vector.tensor_tensor(inv[u][:, 0:S], root[u][:], root[u][:], ALU.mult)
             finish_on_vector(u)
         for u in range(EARLY, TILES):
             inverse_root(u, h_psum[u][0], slice(0, S))
-            nc.scalar.activation(inv[u][:], root[u][:], ACT.Square)
+            nc.scalar.activation(inv[u][:, 0:S], root[u][:], ACT.Square)
         finish_on_vector(2)
         last = TILES - 1
         for half in range(2):

@@ -16,8 +16,10 @@ P = 128
 S = 512
 HALF = S // 2
 TILES = 4
-EARLY = 2
+RUN = 8
+QUADRANT = 32
 SPARE = 32
+EARLY = 2
 FLOPS = 3 * 2 * 512 * 512 * 512
 
 
@@ -32,8 +34,8 @@ def tile_picked_twpqgatebnorm_none_p_kernel(
         sb = ctx.enter_context(tc.tile_pool(name="sb", bufs=1))
         psum = ctx.enter_context(tc.psum_pool(name="psum", bufs=1))
 
-        def tile(name, shape, dtype, tag=None):
-            return sb.tile(shape, dtype, name=name, tag=tag or name, align_bytes=64)
+        def tile(name, shape, dtype, reuse=None):
+            return sb.tile(shape, dtype, name=name, tag=reuse or name, align_bytes=64)
 
         def load_list(name, src):
             dst = sb.tile([P, S // 16], U16, name=name)
@@ -43,7 +45,7 @@ def tile_picked_twpqgatebnorm_none_p_kernel(
         def load_scale_rows(name, src, width):
             dst = tile(name, [P, width], U8)
             rows = src[0].bitcast(I32).rearrange("q (o c) -> q o c", o=1)
-            nc.sync.dma_start(dst[:].bitcast(I32), rows.to_broadcast([16, 8, width // 4]))
+            nc.sync.dma_start(dst[:].bitcast(I32), rows.to_broadcast([P // RUN, RUN, width // 4]))
             return dst
 
         def load_words(name, src, width):
@@ -51,7 +53,7 @@ def tile_picked_twpqgatebnorm_none_p_kernel(
             nc.sync.dma_start(dst[:].bitcast(I32), src[0].rearrange("p c r -> p (c r)").bitcast(I32))
             return dst
 
-        def window(name):
+        def row_with_spare(name):
             dst = tile(name, [P, S + SPARE], F32)
             nc.vector.memset(dst[:, S:], 0.0)
             return dst
@@ -62,8 +64,10 @@ def tile_picked_twpqgatebnorm_none_p_kernel(
         def cols(half):
             return slice(half * HALF, (half + 1) * HALF)
 
-        planes = tile("planes", [P, 4 * S], U8)
-        nc.vector.memset(planes[:].bitcast(I32), 0)
+        d_scale_operand = tile("d_scale_operand", [P, 2 * S], U8)
+        x_scale_operand = tile("x_scale_operand", [P, 2 * S], U8)
+        nc.vector.memset(d_scale_operand[:].bitcast(I32), 0)
+        nc.vector.memset(x_scale_operand[:].bitcast(I32), 0)
 
         warm = tile("warm", [P, 24], F32)
         nc.vector.memset(warm[:, 0:1], 0.0)
@@ -77,19 +81,13 @@ def tile_picked_twpqgatebnorm_none_p_kernel(
         k1_l = load_list("k1_l", k1)
         x_table = load_words("x_table", x_words, tokens)
         d_table = load_words("d_table", d_words, codewords)
-        w_raw = tile("w_raw", [P, TILES, S], F32)
-        w_rows = w1.rearrange("(g t r) m -> t g r m", t=TILES, r=8)
-        for t in range(TILES - 1):
-            nc.sync.dma_start(w_raw[:, t, :], w_rows[t])
-        gain_raw = tile("gain_raw", [P, TILES, 8], F32)
-        gain_rows = gn.rearrange("(g t r) o -> t g r o", t=TILES, r=8)
-        with nc.allow_non_contiguous_dma(reason="one gain a partition"):
-            for t in range(TILES):
-                nc.sync.dma_start(gain_raw[:, t, 0:1], gain_rows[t])
-        nc.sync.dma_start(w_raw[:, TILES - 1, :], w_rows[TILES - 1])
         n2_l = load_list("n2_l", n2)
         n1_l = load_list("n1_l", n1)
         n3_l = load_list("n3_l", n3)
+        w_raw = tile("w_raw", [P, TILES, S], F32)
+        w_rows = w1.rearrange("(g t r) m -> t g r m", t=TILES, r=RUN)
+        for t in range(TILES):
+            nc.sync.dma_start(w_raw[:, t, :], w_rows[t])
 
         d_bytes_picked = tile("d_bytes_picked", [P, 2 * S], U8)
         x_bytes_picked = tile("x_bytes_picked", [P, 2 * S], U8)
@@ -97,40 +95,44 @@ def tile_picked_twpqgatebnorm_none_p_kernel(
         nc.vector.tensor_copy(x_bytes_picked[:, S : 2 * S], x_bytes[:].indirect(offs_l[:]))
         nc.vector.tensor_copy(d_bytes_picked[:, 0:S], d_bytes[:].indirect(k2_l[:]))
         nc.vector.tensor_copy(d_bytes_picked[:, S : 2 * S], d_bytes[:].indirect(k1_l[:]))
-        staged = tile("staged", [P, 4 * S], U8)
+        d_bytes_dealt = tile("d_bytes_dealt", [P, 2 * S], U8)
         nc.vector.tensor_copy(
-            staged[:, 0 : 2 * S].bitcast(I32).rearrange("p (l t g r) -> p l t g r", l=2, t=TILES, r=2),
-            d_bytes_picked[:].bitcast(I32).rearrange("p (l g t r) -> p l t g r", l=2, t=TILES, r=2),
+            d_bytes_dealt[:].bitcast(I32).rearrange("p (l t g w) -> p l t g w", l=2, t=TILES, w=RUN // 4),
+            d_bytes_picked[:].bitcast(I32).rearrange("p (l g t w) -> p l t g w", l=2, t=TILES, w=RUN // 4),
         )
-        nc.vector.tensor_copy(staged[:, 2 * S : 4 * S].bitcast(I32), x_bytes_picked[:].bitcast(I32))
-        for q in range(4):
-            nc.sync.dma_start(
-                planes[32 * q : 32 * q + 4, :].bitcast(I32),
-                staged[32 * q : 32 * q + 32 : 8, :].bitcast(I32),
-            )
+        for operand, picked in ((x_scale_operand, x_bytes_picked), (d_scale_operand, d_bytes_dealt)):
+            for q0 in range(0, P, QUADRANT):
+                nc.sync.dma_start(
+                    operand[q0 : q0 + QUADRANT // RUN, :].bitcast(I32),
+                    picked[q0 : q0 + QUADRANT : RUN, :].bitcast(I32),
+                )
 
+        gain_raw = tile("gain_raw", [P, TILES, 8], F32, reuse="d_bytes_picked")
+        gain_rows = gn.rearrange("(g t r) o -> t g r o", t=TILES, r=RUN)
+        with nc.allow_non_contiguous_dma(reason="one gain a partition"):
+            for t in range(TILES):
+                nc.sync.dma_start(gain_raw[:, t, 0:1], gain_rows[t])
         gain = tile("gain", [P, TILES], F32)
-        nc.scalar.activation(gain[:], gain_raw[:, :, 0], ACT.Copy, scale=0.0625)
 
-        def coded_layer(which, name, d_list, x_list, d_tag, x_tag):
-            x_picked = tile(name + "_x", [P, S], U32, x_tag)
-            d_picked = tile(name + "_d", [P, S], U32, d_tag)
-            d_dealt = tile(name + "_dealt", [P, S], U32)
+        def coded_layer(layer, name, d_list, x_list, d_reuse=None, x_reuse=None):
+            x_picked = tile(name + "_x_picked", [P, S], U32, reuse=x_reuse)
+            d_picked = tile(name + "_d_picked", [P, S], U32, reuse=d_reuse)
+            d_dealt = tile(name + "_d_dealt", [P, S], U32)
             nc.vector.tensor_copy(x_picked[:], x_table[:].indirect(x_list[:]))
             nc.vector.tensor_copy(d_picked[:], d_table[:].indirect(d_list[:]))
             nc.vector.tensor_copy(
-                d_dealt[:].rearrange("p (t g r) -> p t g r", t=TILES, r=8),
-                d_picked[:].rearrange("p (g t r) -> p t g r", t=TILES, r=8),
+                d_dealt[:].rearrange("p (t g r) -> p t g r", t=TILES, r=RUN),
+                d_picked[:].rearrange("p (g t r) -> p t g r", t=TILES, r=RUN),
             )
             banks = []
             for t in range(TILES):
-                bank = psum.tile([P, S], F32, name=name + str(t), tag="bank" + str(TILES * which + t))
+                bank = psum.tile([P, S], F32, name=name + str(t), tag="bank" + str(TILES * layer + t))
                 nc.tensor.matmul_mx(
                     out=bank[:],
                     lhsT=d_dealt[:, P * t : P * (t + 1)].bitcast(FP8X4),
-                    lhsT_scale=planes[:, which * S + P * t : which * S + P * (t + 1)],
+                    lhsT_scale=d_scale_operand[:, layer * S + P * t : layer * S + P * (t + 1)],
                     rhs=x_picked[:].bitcast(FP8X4),
-                    rhs_scale=planes[:, (2 + which) * S : (3 + which) * S],
+                    rhs_scale=x_scale_operand[:, layer * S : (layer + 1) * S],
                     start=True,
                     stop=True,
                 )
@@ -138,46 +140,49 @@ def tile_picked_twpqgatebnorm_none_p_kernel(
             return banks
 
         w_bf = tile("w_bf", [P, TILES * S], BF16)
-        w_src = w_raw[:].rearrange("p t (g u h i) -> p u g h t i", u=TILES, h=4, i=2)
+        w_src = w_raw[:].rearrange("p t (g u c e) -> p u g c t e", u=TILES, c=RUN // 2, e=2)
         for u in range(TILES):
             nc.scalar.copy(
-                w_bf[:, u * S : (u + 1) * S].rearrange("p (g h i t) -> p g h t i", h=4, i=2, t=TILES),
+                w_bf[:, u * S : (u + 1) * S].rearrange("p (g c e t) -> p g c t e", c=RUN // 2, e=2, t=TILES),
                 w_src[:, u],
             )
 
-        b_banks = coded_layer(0, "b", k2_l, two_l, "b_d", "b_x")
-        gate = [window("gate" + str(t)) for t in range(TILES)]
+        b_banks = coded_layer(0, "b", k2_l, two_l)
+        gate = [row_with_spare("gate" + str(t)) for t in range(TILES)]
         for t in range(TILES):
             nc.scalar.activation(gate[t][:, 0:S], b_banks[t][:], ACT.Sigmoid, scale=0.0625)
 
-        a_banks = coded_layer(1, "a", k1_l, offs_l, "b_d", "staged")
+        nc.scalar.activation(gain[:], gain_raw[:, :, 0], ACT.Copy, scale=0.0625)
+        nc.scalar.activation(warm[:, 16:17], gate[TILES - 1][:, S - 1 : S], ACT.Abs_reciprocal_sqrt, bias=0.5)
+
+        a_banks = coded_layer(1, "a", k1_l, offs_l, d_reuse="b_d_picked", x_reuse="d_bytes_dealt")
         w_codes = tile("w_codes", [P, S], U32)
         w_scales = tile("w_scales", [P, S], U8)
         nc.vector.quantize_mx(out=w_codes[:].bitcast(FP8X4), scales=w_scales[:], in_=w_bf[:])
         ga = [tile("ga" + str(t), [P, S], F32) for t in range(TILES)]
-        for t in range(TILES):
+        nc.vector.tensor_scalar(ga[0][:], a_banks[0][:], gain[:, 0:1], None, ALU.mult)
+        for t in range(1, TILES):
             nc.scalar.activation(ga[t][:], a_banks[t][:], ACT.Copy, scale=gain[:, t : t + 1])
 
         gated = tile("gated", [P, TILES, S], F32)
-        other = [tile("other" + str(half), [P, TILES, HALF], F32) for half in range(2)]
+        moved = [tile("moved" + str(half), [P, TILES, HALF], F32) for half in range(2)]
         for half in range(2):
             for t in range(TILES):
-                nc.scalar.activation(other[half][:, t, :], ga[t][:].indirect(half_of(n1_l, half)), ACT.Copy, scale=-0.5)
+                nc.scalar.activation(moved[half][:, t, :], ga[t][:].indirect(half_of(n1_l, half)), ACT.Copy, scale=-0.5)
         for t in range(TILES):
             nc.vector.tensor_tensor(gated[:, t, :], gate[t][:].indirect(n2_l[:]), ga[t][:], ALU.mult)
 
-        nc.scalar.activation(warm[:, 16:17], other[1][:, TILES - 1, HALF - 1 : HALF], ACT.Abs_reciprocal_sqrt, bias=0.5)
         h_psum = []
         for u in range(TILES):
             first = psum.tile([P, S], F32, name="h" + str(u), tag="bank" + str(u))
-            second = psum.tile([P, S], F32, name="hh" + str(u), tag="bank" + str(TILES + u)) if u < EARLY else first
+            second = psum.tile([P, S], F32, name="h_late" + str(u), tag="bank" + str(TILES + u)) if u < EARLY else first
             h_psum.append([first, second])
         for half in range(2):
-            z_bf = tile("z_bf" + str(half), [P, TILES * HALF], BF16, "z_bf")
+            z_bf = tile("z_bf" + str(half), [P, TILES * HALF], BF16, reuse="z_bf0")
             nc.vector.tensor_tensor(
-                z_bf[:].rearrange("p (c i t) -> p c t i", i=2, t=TILES),
-                gated[:, :, cols(half)].rearrange("p t (c i) -> p c t i", i=2),
-                other[half][:].rearrange("p t (c i) -> p c t i", i=2),
+                z_bf[:].rearrange("p (c e t) -> p c t e", e=2, t=TILES),
+                gated[:, :, cols(half)].rearrange("p t (c e) -> p c t e", e=2),
+                moved[half][:].rearrange("p t (c e) -> p c t e", e=2),
                 ALU.add,
             )
             z_codes = tile("z_codes" + str(half), [P, HALF], U32)
@@ -194,37 +199,40 @@ def tile_picked_twpqgatebnorm_none_p_kernel(
                     stop=True,
                 )
 
+        last = TILES - 1
         root = [tile("root" + str(u), [P, S], F32) for u in range(TILES)]
         inv = [tile("inv" + str(u), [P, 2 * S], F32) for u in range(TILES)]
         size = [inv[u][:, S : 2 * S] for u in range(TILES)]
-        side = [tile("side" + str(u), [P, S], F32) for u in range(TILES)]
+        h_copy = [tile("h_copy" + str(u), [P, S], F32) for u in range(last)]
+        inv_picked = tile("inv_picked", [P, S], F32)
         res = [tile("res" + str(u), [P, S], F32) for u in range(TILES)]
-        out_rows = out.rearrange("(g u r) j -> u g r j", u=TILES, r=8)
+        out_rows = out.rearrange("(g u r) j -> u g r j", u=TILES, r=RUN)
 
         def inverse_root(u, bank, span):
             nc.scalar.activation(size[u][:, span], bank[:, span], ACT.Abs)
             nc.scalar.activation(root[u][:, span], size[u][:, span], ACT.Abs_reciprocal_sqrt, bias=0.5)
 
         def finish_on_vector(u):
-            nc.vector.tensor_tensor(res[u][:], inv[u][:].indirect(n3_l[:]), side[u][:], ALU.mult)
+            nc.vector.tensor_tensor(res[u][:], inv[u][:].indirect(n3_l[:]), h_copy[u][:], ALU.mult)
             nc.sync.dma_start(out_rows[u], res[u][:])
 
-        for half in range(2):
+        for half, copy in enumerate((nc.scalar.copy, nc.vector.tensor_copy)):
             for u in range(EARLY):
                 inverse_root(u, h_psum[u][half], cols(half))
-                nc.vector.tensor_copy(side[u][:, cols(half)], h_psum[u][half][:, cols(half)])
-        nc.vector.tensor_copy(side[2][:], h_psum[2][0][:])
+                copy(h_copy[u][:, cols(half)], h_psum[u][half][:, cols(half)])
+        for u in range(EARLY, last):
+            nc.vector.tensor_copy(h_copy[u][:], h_psum[u][0][:])
         for u in range(EARLY):
             nc.vector.tensor_tensor(inv[u][:, 0:S], root[u][:], root[u][:], ALU.mult)
             finish_on_vector(u)
         for u in range(EARLY, TILES):
             inverse_root(u, h_psum[u][0], slice(0, S))
             nc.scalar.activation(inv[u][:, 0:S], root[u][:], ACT.Square)
-        finish_on_vector(2)
-        last = TILES - 1
+        for u in range(EARLY, last):
+            finish_on_vector(u)
         for half in range(2):
-            nc.scalar.activation(side[last][:, cols(half)], inv[last][:].indirect(half_of(n3_l, half)), ACT.Copy)
+            nc.scalar.activation(inv_picked[:, cols(half)], inv[last][:].indirect(half_of(n3_l, half)), ACT.Copy)
             nc.vector.tensor_tensor(
-                res[last][:, cols(half)], h_psum[last][0][:, cols(half)], side[last][:, cols(half)], ALU.mult
+                res[last][:, cols(half)], h_psum[last][0][:, cols(half)], inv_picked[:, cols(half)], ALU.mult
             )
             nc.sync.dma_start(out_rows[last][:, :, cols(half)], res[last][:, cols(half)])

from contextlib import ExitStack

import concourse.mybir as mybir

F32 = mybir.dt.float32
BF16 = mybir.dt.bfloat16
I32 = mybir.dt.int32
U32 = mybir.dt.uint32
U16 = mybir.dt.uint16
U8 = mybir.dt.uint8
FP8X4 = mybir.dt.float8_e4m3fn_x4
ACT = mybir.ActivationFunctionType
ALU = mybir.AluOpType

P = 128
S = 512
HALF = S // 2
TILES = 4
RUN = 8
QUADRANT = 32
SPARE = 32
EARLY = 2
FLOPS = 3 * 2 * 512 * 512 * 512


def tile_picked_twpqgatebnorm_none_p_kernel(
    tc, x_words, x_scales, d_words, d_scales, gn, w1, offs, k1, two, k2, n1, n2, n3, out
):
    nc = tc.nc
    tokens = x_words.shape[2]
    codewords = d_words.shape[2]

    with ExitStack() as ctx:
        sb = ctx.enter_context(tc.tile_pool(name="sb", bufs=1))
        psum = ctx.enter_context(tc.psum_pool(name="psum", bufs=1))

        def tile(name, shape, dtype, reuse=None):
            return sb.tile(shape, dtype, name=name, tag=reuse or name, align_bytes=64)

        def load_list(name, src):
            dst = sb.tile([P, S // 16], U16, name=name)
            nc.sync.dma_start(dst[:], src)
            return dst

        def load_scale_rows(name, src, width):
            dst = tile(name, [P, width], U8)
            rows = src[0].bitcast(I32).rearrange("q (o c) -> q o c", o=1)
            nc.sync.dma_start(dst[:].bitcast(I32), rows.to_broadcast([P // RUN, RUN, width // 4]))
            return dst

        def load_words(name, src, width):
            dst = tile(name, [P, width], U32)
            nc.sync.dma_start(dst[:].bitcast(I32), src[0].rearrange("p c r -> p (c r)").bitcast(I32))
            return dst

        def row_with_spare(name):
            dst = tile(name, [P, S + SPARE], F32)
            nc.vector.memset(dst[:, S:], 0.0)
            return dst

        def half_of(lst, half):
            return lst[:, half * (HALF // 16) : (half + 1) * (HALF // 16)]

        def cols(half):
            return slice(half * HALF, (half + 1) * HALF)

        d_scale_operand = tile("d_scale_operand", [P, 2 * S], U8)
        x_scale_operand = tile("x_scale_operand", [P, 2 * S], U8)
        nc.vector.memset(d_scale_operand[:].bitcast(I32), 0)
        nc.vector.memset(x_scale_operand[:].bitcast(I32), 0)

        warm = tile("warm", [P, 24], F32)
        nc.vector.memset(warm[:, 0:1], 0.0)
        nc.scalar.activation(warm[:, 8:9], warm[:, 0:1], ACT.Sigmoid)

        two_l = load_list("two_l", two)
        x_bytes = load_scale_rows("x_bytes", x_scales, tokens)
        offs_l = load_list("offs_l", offs)
        d_bytes = load_scale_rows("d_bytes", d_scales, codewords)
        k2_l = load_list("k2_l", k2)
        k1_l = load_list("k1_l", k1)
        x_table = load_words("x_table", x_words, tokens)
        d_table = load_words("d_table", d_words, codewords)
        n2_l = load_list("n2_l", n2)
        n1_l = load_list("n1_l", n1)
        n3_l = load_list("n3_l", n3)
        w_raw = tile("w_raw", [P, TILES, S], F32)
        w_rows = w1.rearrange("(g t r) m -> t g r m", t=TILES, r=RUN)
        for t in range(TILES):
            nc.sync.dma_start(w_raw[:, t, :], w_rows[t])

        d_bytes_picked = tile("d_bytes_picked", [P, 2 * S], U8)
        x_bytes_picked = tile("x_bytes_picked", [P, 2 * S], U8)
        nc.vector.tensor_copy(x_bytes_picked[:, 0:S], x_bytes[:].indirect(two_l[:]))
        nc.vector.tensor_copy(x_bytes_picked[:, S : 2 * S], x_bytes[:].indirect(offs_l[:]))
        nc.vector.tensor_copy(d_bytes_picked[:, 0:S], d_bytes[:].indirect(k2_l[:]))
        nc.vector.tensor_copy(d_bytes_picked[:, S : 2 * S], d_bytes[:].indirect(k1_l[:]))
        d_bytes_dealt = tile("d_bytes_dealt", [P, 2 * S], U8)
        nc.vector.tensor_copy(
            d_bytes_dealt[:].bitcast(I32).rearrange("p (l t g w) -> p l t g w", l=2, t=TILES, w=RUN // 4),
            d_bytes_picked[:].bitcast(I32).rearrange("p (l g t w) -> p l t g w", l=2, t=TILES, w=RUN // 4),
        )
        for operand, picked in ((x_scale_operand, x_bytes_picked), (d_scale_operand, d_bytes_dealt)):
            for q0 in range(0, P, QUADRANT):
                nc.sync.dma_start(
                    operand[q0 : q0 + QUADRANT // RUN, :].bitcast(I32),
                    picked[q0 : q0 + QUADRANT : RUN, :].bitcast(I32),
                )

        gain_raw = tile("gain_raw", [P, TILES, 8], F32, reuse="d_bytes_picked")
        gain_rows = gn.rearrange("(g t r) o -> t g r o", t=TILES, r=RUN)
        with nc.allow_non_contiguous_dma(reason="one gain a partition"):
            for t in range(TILES):
                nc.sync.dma_start(gain_raw[:, t, 0:1], gain_rows[t])
        gain = tile("gain", [P, TILES], F32)

        def coded_layer(layer, name, d_list, x_list, d_reuse=None, x_reuse=None):
            x_picked = tile(name + "_x_picked", [P, S], U32, reuse=x_reuse)
            d_picked = tile(name + "_d_picked", [P, S], U32, reuse=d_reuse)
            d_dealt = tile(name + "_d_dealt", [P, S], U32)
            nc.vector.tensor_copy(x_picked[:], x_table[:].indirect(x_list[:]))
            nc.vector.tensor_copy(d_picked[:], d_table[:].indirect(d_list[:]))
            nc.vector.tensor_copy(
                d_dealt[:].rearrange("p (t g r) -> p t g r", t=TILES, r=RUN),
                d_picked[:].rearrange("p (g t r) -> p t g r", t=TILES, r=RUN),
            )
            banks = []
            for t in range(TILES):
                bank = psum.tile([P, S], F32, name=name + str(t), tag="bank" + str(TILES * layer + t))
                nc.tensor.matmul_mx(
                    out=bank[:],
                    lhsT=d_dealt[:, P * t : P * (t + 1)].bitcast(FP8X4),
                    lhsT_scale=d_scale_operand[:, layer * S + P * t : layer * S + P * (t + 1)],
                    rhs=x_picked[:].bitcast(FP8X4),
                    rhs_scale=x_scale_operand[:, layer * S : (layer + 1) * S],
                    start=True,
                    stop=True,
                )
                banks.append(bank)
            return banks

        w_bf = tile("w_bf", [P, TILES * S], BF16)
        w_src = w_raw[:].rearrange("p t (g u c e) -> p u g c t e", u=TILES, c=RUN // 2, e=2)
        for u in range(TILES):
            nc.scalar.copy(
                w_bf[:, u * S : (u + 1) * S].rearrange("p (g c e t) -> p g c t e", c=RUN // 2, e=2, t=TILES),
                w_src[:, u],
            )

        b_banks = coded_layer(0, "b", k2_l, two_l)
        gate = [row_with_spare("gate" + str(t)) for t in range(TILES)]
        for t in range(TILES):
            nc.scalar.activation(gate[t][:, 0:S], b_banks[t][:], ACT.Sigmoid, scale=0.0625)

        nc.scalar.activation(gain[:], gain_raw[:, :, 0], ACT.Copy, scale=0.0625)
        nc.scalar.activation(warm[:, 16:17], gate[TILES - 1][:, S - 1 : S], ACT.Abs_reciprocal_sqrt, bias=0.5)

        a_banks = coded_layer(1, "a", k1_l, offs_l, d_reuse="b_d_picked", x_reuse="d_bytes_dealt")
        w_codes = tile("w_codes", [P, S], U32)
        w_scales = tile("w_scales", [P, S], U8)
        nc.vector.quantize_mx(out=w_codes[:].bitcast(FP8X4), scales=w_scales[:], in_=w_bf[:])
        ga = [tile("ga" + str(t), [P, S], F32) for t in range(TILES)]
        nc.vector.tensor_scalar(ga[0][:], a_banks[0][:], gain[:, 0:1], None, ALU.mult)
        for t in range(1, TILES):
            nc.scalar.activation(ga[t][:], a_banks[t][:], ACT.Copy, scale=gain[:, t : t + 1])

        gated = tile("gated", [P, TILES, S], F32)
        moved = [tile("moved" + str(half), [P, TILES, HALF], F32) for half in range(2)]
        for half in range(2):
            for t in range(TILES):
                nc.scalar.activation(moved[half][:, t, :], ga[t][:].indirect(half_of(n1_l, half)), ACT.Copy, scale=-0.5)
        for t in range(TILES):
            nc.vector.tensor_tensor(gated[:, t, :], gate[t][:].indirect(n2_l[:]), ga[t][:], ALU.mult)

        h_psum = []
        for u in range(TILES):
            first = psum.tile([P, S], F32, name="h" + str(u), tag="bank" + str(u))
            second = psum.tile([P, S], F32, name="h_late" + str(u), tag="bank" + str(TILES + u)) if u < EARLY else first
            h_psum.append([first, second])
        for half in range(2):
            z_bf = tile("z_bf" + str(half), [P, TILES * HALF], BF16, reuse="z_bf0")
            nc.vector.tensor_tensor(
                z_bf[:].rearrange("p (c e t) -> p c t e", e=2, t=TILES),
                gated[:, :, cols(half)].rearrange("p t (c e) -> p c t e", e=2),
                moved[half][:].rearrange("p t (c e) -> p c t e", e=2),
                ALU.add,
            )
            z_codes = tile("z_codes" + str(half), [P, HALF], U32)
            z_scales = tile("z_scales" + str(half), [P, HALF], U8)
            nc.vector.quantize_mx(out=z_codes[:].bitcast(FP8X4), scales=z_scales[:], in_=z_bf[:])
            for u in range(TILES):
                nc.tensor.matmul_mx(
                    out=h_psum[u][half][:, cols(half)],
                    lhsT=w_codes[:, P * u : P * (u + 1)].bitcast(FP8X4),
                    lhsT_scale=w_scales[:, P * u : P * (u + 1)],
                    rhs=z_codes[:].bitcast(FP8X4),
                    rhs_scale=z_scales[:],
                    start=True,
                    stop=True,
                )

        last = TILES - 1
        root = [tile("root" + str(u), [P, S], F32) for u in range(TILES)]
        inv = [tile("inv" + str(u), [P, 2 * S], F32) for u in range(TILES)]
        size = [inv[u][:, S : 2 * S] for u in range(TILES)]
        h_copy = [tile("h_copy" + str(u), [P, S], F32) for u in range(last)]
        inv_picked = tile("inv_picked", [P, S], F32)
        res = [tile("res" + str(u), [P, S], F32) for u in range(TILES)]
        out_rows = out.rearrange("(g u r) j -> u g r j", u=TILES, r=RUN)

        def inverse_root(u, bank, span):
            nc.scalar.activation(size[u][:, span], bank[:, span], ACT.Abs)
            nc.scalar.activation(root[u][:, span], size[u][:, span], ACT.Abs_reciprocal_sqrt, bias=0.5)

        def finish_on_vector(u):
            nc.vector.tensor_tensor(res[u][:], inv[u][:].indirect(n3_l[:]), h_copy[u][:], ALU.mult)
            nc.sync.dma_start(out_rows[u], res[u][:])

        for half, copy in enumerate((nc.scalar.copy, nc.vector.tensor_copy)):
            for u in range(EARLY):
                inverse_root(u, h_psum[u][half], cols(half))
                copy(h_copy[u][:, cols(half)], h_psum[u][half][:, cols(half)])
        for u in range(EARLY, last):
            nc.vector.tensor_copy(h_copy[u][:], h_psum[u][0][:])
        for u in range(EARLY):
            nc.vector.tensor_tensor(inv[u][:, 0:S], root[u][:], root[u][:], ALU.mult)
            finish_on_vector(u)
        for u in range(EARLY, TILES):
            inverse_root(u, h_psum[u][0], slice(0, S))
            nc.scalar.activation(inv[u][:, 0:S], root[u][:], ACT.Square)
        for u in range(EARLY, last):
            finish_on_vector(u)
        for half in range(2):
            nc.scalar.activation(inv_picked[:, cols(half)], inv[last][:].indirect(half_of(n3_l, half)), ACT.Copy)
            nc.vector.tensor_tensor(
                res[last][:, cols(half)], h_psum[last][0][:, cols(half)], inv_picked[:, cols(half)], ALU.mult
            )
            nc.sync.dma_start(out_rows[last][:, :, cols(half)], res[last][:, cols(half)])
